import numpy as np
import ml_dtypes


def mxq(x, axis, fmt="e4m3"):
    dtype, down = {"e4m3": (ml_dtypes.float8_e4m3fn, 7), "e5m2": (ml_dtypes.float8_e5m2, 14)}[fmt]
    v = np.moveaxis(np.asarray(x, np.float32).astype(ml_dtypes.bfloat16).astype(np.float64), axis, -1)
    blocks = v.reshape(v.shape[:-1] + (-1, 32))
    amax = np.abs(blocks).max(-1, keepdims=True)
    byte = np.maximum(np.where(amax > 0, np.frexp(amax)[1] - 1 + 127, 0) - down, 1)
    scale = np.exp2(byte - 127.0)
    codes = (blocks / scale).astype(np.float32).astype(dtype).astype(np.float64)
    return np.moveaxis((codes * scale).reshape(v.shape), -1, axis)


WIDE = False


def mx_kscale(k):
    if not WIDE:
        return np.ones(k)
    levels = np.array([10, -10, 5, -5, 0])
    if k % 512:
        return np.exp2(np.random.permutation(np.resize(levels, k // 32))).repeat(32)
    a = np.empty((k // 512, 16))
    for p in range(k // 512):
        a[p, :8] = np.random.permutation(np.resize(levels, 8))
        for g in range(8):
            far = levels[np.abs(levels - a[p, g]) >= 10]
            a[p, g + 8] = far[np.random.randint(len(far))]
    return np.exp2(a.ravel()).repeat(32)


def f64(x):
    return np.asarray(x).astype(np.float64)


def striped(idx):
    return np.tile(idx.reshape(-1, 16).T, (8, 1)).astype(np.uint16)


def unstriped(offs):
    return offs[:16].T.reshape(-1).astype(np.int64)


E2M1 = np.array([0.0, 0.5, 1.0, 1.5, 2.0, 3.0, 4.0, 6.0, -0.0, -0.5, -1.0, -1.5, -2.0, -3.0, -4.0, -6.0])


def pack_weight(w, fmt):
    k, n = w.shape
    w = f64(np.asarray(w, np.float32).astype(ml_dtypes.bfloat16)).reshape(k // 32, 32, n)
    amax = np.abs(w).max(1)
    if fmt == "e4m3":
        byte = np.frexp(amax)[1] - 1 + 127 - 7
    else:
        mant, ex = np.frexp(amax / 6.0)
        byte = np.where(mant > 0.5, ex, ex - 1) + 127
    byte = np.clip(np.where(amax > 0, byte, 1), 1, 254)
    scaled = (w * np.exp2(127.0 - byte)[:, None, :]).reshape(k, n).astype(np.float32)
    by_word = np.ascontiguousarray(scaled.reshape(k // 512, 128, 4, n).transpose(0, 1, 3, 2))
    if fmt == "e4m3":
        words = by_word.astype(ml_dtypes.float8_e4m3fn).view(np.uint8)
    else:
        c = by_word.astype(ml_dtypes.float4_e2m1fn).view(np.uint8) & 0xF
        words = (c[..., 0::2] | (c[..., 1::2] << 4)).reshape(k // 512, 128, 2 * n)
    return np.ascontiguousarray(words), np.ascontiguousarray(byte.astype(np.uint8).reshape(k // 512, 16, n))


def unpack_weight(words, scales, fmt):
    g, _, n = scales.shape
    words = np.ascontiguousarray(words).reshape(g, 128, n, -1)
    if fmt == "e4m3":
        vals = words.view(ml_dtypes.float8_e4m3fn).astype(np.float64)
    else:
        nib = np.empty((g, 128, n, 4), np.uint8)
        nib[..., 0::2] = words & 0xF
        nib[..., 1::2] = words >> 4
        vals = E2M1[nib]
    vals = vals * np.repeat(np.exp2(scales.astype(np.float64) - 127.0), 8, axis=1)[..., None]
    return vals.transpose(0, 1, 3, 2).reshape(g * 512, n)


def pack_table(v):
    words, scales = pack_weight(v, "e4m3")
    return np.concatenate([words.reshape(words.shape[0], -1), scales.reshape(scales.shape[0], -1)], axis=1)


def unpack_table(tab):
    g, t = tab.shape[0], tab.shape[1] // 528
    return unpack_weight(tab[:, :512 * t].reshape(g, 128, t, 4), tab[:, 512 * t:].reshape(g, 16, t), "e4m3")


K, M, T, S = 512, 256, 2048, 1024


def setup_inputs():
    n = np.random.standard_normal
    s = mx_kscale(K)[:, None]
    s2 = mx_kscale(512)[:, None]
    p_w4 = pack_weight(n((K, M)) / np.sqrt(K) / s, "e2m1")
    return {
        "tab": pack_table(n((K, T)) * s),
        "w4_words": p_w4[0],
        "w4_scales": p_w4[1],
        "c": (n((512, S)) * s2).astype(np.float32),
        "u": (n((512, M)) / np.sqrt(512) / s2).astype(np.float32),
        "b": (0.3 * n(256)).astype(np.float32),
        "wgo": np.tile(np.random.uniform(0.5, 2.0, S), (128, 1)).astype(np.float32),
        "offs": striped(np.random.permutation(T)[:S]),
        "offs2": striped(np.random.permutation(T)[:S]),
    }


def reference(tab, w4_words, w4_scales, c, u, b, wgo, offs, offs2):
    tab_ = unpack_table(tab)[:, unstriped(offs)]
    w4_ = unpack_weight(w4_words, w4_scales, "e2m1")
    c_ = mxq(f64(c), 0, "e4m3")
    u_ = mxq(f64(u), 0, "e4m3")
    y = w4_.T @ tab_ + u_.T @ c_
    out = np.zeros((M, T))
    out[:, unstriped(offs2)] = f64(wgo)[0] * (y + f64(b)[:, None])
    return out

@@ -1,0 +1,154 @@
+from contextlib import ExitStack
+
+import concourse.mybir as mybir
+
+K, M, T, S = 512, 256, 2048, 1024
+FLOPS = 2 * 2 * K * M * S
+
+F32 = mybir.dt.float32
+BF16 = mybir.dt.bfloat16
+I32 = mybir.dt.int32
+U32 = mybir.dt.uint32
+U16 = mybir.dt.uint16
+U8 = mybir.dt.uint8
+FP8X4 = mybir.dt.float8_e4m3fn_x4
+FP4X4 = mybir.dt.float4_e2m1fn_x4
+
+P = 128
+PACK = 4
+QUADS = 4
+CHUNKS = [(0, 256), (256, 512), (512, 1024)]
+GATHERS = [(0, 256), (256, 1024)]
+
+
+def interleave(nc, grouped, raw):
+    nc.scalar.copy(
+        out=grouped.rearrange("p (c i) t -> p c t i", i=4),
+        in_=raw.rearrange("p t (c i) -> p c t i", i=4),
+    )
+
+
+def tile_list_tabscat_d_bias_kernel(tc, tab, w4_words, w4_scales, c, u, b, wgo, offs, offs2, out):
+    nc = tc.nc
+    mult = mybir.AluOpType.mult
+    ident = mybir.ActivationFunctionType.Identity
+    with ExitStack() as ctx:
+        keep = ctx.enter_context(tc.tile_pool(name="keep", bufs=1))
+        psum = ctx.enter_context(tc.psum_pool(name="psum", bufs=1))
+
+        idx = keep.tile([P, S // 16], U16, name="idx")
+        idx2 = keep.tile([P, S // 16], U16, name="idx2")
+        tab_words = keep.tile([P, T], I32, name="tab_words", align_bytes=64)
+        tab_plane = keep.tile([P, T], U8, name="tab_plane", align_bytes=64)
+        w4_codes = keep.tile([P, 2 * M], U8, name="w4_codes", align_bytes=64)
+        w4_plane = keep.tile([P, M], U8, name="w4_plane", align_bytes=64)
+        bias = keep.tile([P, 2], F32, name="bias")
+        u_raw = keep.tile([P, PACK, M], F32, name="u_raw", align_bytes=64)
+        pages = [keep.tile([P, T], F32, name="page%d" % m, align_bytes=64) for m in range(2)]
+
+        nc.vector.memset(tab_plane[:].bitcast(I32), 0)
+        nc.vector.memset(w4_plane[:].bitcast(I32), 0)
+        for page in pages:
+            nc.vector.memset(page[:], 0.0)
+
+        tab_i32 = tab[0].bitcast(I32)
+        tab_rows = tab_i32[P * T :].rearrange("(q r t) -> r q t", q=QUADS, r=4)
+        w4_rows = w4_scales[0].bitcast(I32).rearrange("(q r) n -> r q n", q=QUADS)
+        c_view = c.rearrange("(p t) j -> p t j", t=PACK)
+
+        with nc.allow_non_contiguous_dma(reason="one bias value for each partition"):
+            nc.gpsimd.dma_start(out=bias[:], in_=b.rearrange("(m p) -> p m", p=P))
+        nc.gpsimd.dma_start(out=w4_codes[:].bitcast(I32), in_=w4_words[0].bitcast(I32))
+
+        nc.sync.dma_start(idx[:], offs)
+        nc.sync.dma_start(out=tab_words[:], in_=tab_i32[: P * T].rearrange("(p t) -> p t", p=P))
+        for r in range(4):
+            nc.sync.dma_start(out=tab_plane[r:P:32, :].bitcast(I32), in_=tab_rows[r])
+        nc.sync.dma_start(out=u_raw[:], in_=u.rearrange("(p t) n -> p t n", t=PACK))
+        c_raw = []
+        for n, (lo, hi) in enumerate(CHUNKS):
+            c_raw.append(keep.tile([P, PACK, hi - lo], F32, name="c_raw%d" % n, align_bytes=64))
+        wgo_a = keep.tile([P, 256], F32, name="wgo_a", align_bytes=64)
+        wgo_b = keep.tile([P, S - 256], F32, name="wgo_b", align_bytes=64)
+        nc.sync.dma_start(out=c_raw[0][:], in_=c_view[:, :, 0:256])
+        nc.sync.dma_start(idx2[:], offs2)
+        nc.sync.dma_start(out=wgo_a[:], in_=wgo[:, 0:256])
+        for r in range(4):
+            nc.sync.dma_start(out=w4_plane[r:P:32, :].bitcast(I32), in_=w4_rows[r])
+        nc.sync.dma_start(out=c_raw[1][:], in_=c_view[:, :, 256:512])
+        nc.sync.dma_start(out=wgo_b[:], in_=wgo[:, 256:S])
+        nc.sync.dma_start(out=c_raw[2][:], in_=c_view[:, :, 512:S])
+
+        got_words = keep.tile([P, S], U32, name="got_words", align_bytes=64)
+        got_plane = keep.tile([P, S], U8, name="got_plane", align_bytes=64)
+
+        def gather(lo, hi):
+            part = idx[:, lo // 16 : hi // 16]
+            nc.vector.tensor_copy(got_words[:, lo:hi], tab_words[:].bitcast(U32).indirect(part))
+            nc.vector.tensor_copy(got_plane[:, lo:hi], tab_plane[:].indirect(part))
+
+        def quantize(name, raw, width):
+            grouped = keep.tile([P, width, PACK], BF16, name=name + "_bf", align_bytes=64)
+            codes = keep.tile([P, width], U32, name=name + "_codes", align_bytes=64)
+            plane = keep.tile([P, width], U8, name=name + "_plane", align_bytes=64)
+            for lo in range(0, width, 256):
+                hi = min(lo + 256, width)
+                interleave(nc, grouped[:, lo:hi, :], raw[:, :, lo:hi])
+            nc.vector.quantize_mx(
+                out=codes[:].bitcast(FP8X4), scales=plane[:], in_=grouped[:].rearrange("p w t -> p (w t)")
+            )
+            return codes, plane
+
+        def project(m, n, u_q, c_q):
+            lo, hi = CHUNKS[n]
+            acc = psum.tile([P, hi - lo], F32, name="acc%d_%d" % (m, n))
+            step = 512 if hi - lo == 512 else 128
+            for j in range(lo, hi, step):
+                nc.tensor.matmul_mx(
+                    out=acc[:, j - lo : j - lo + step],
+                    lhsT=w4_codes[:, 2 * P * m : 2 * P * (m + 1)].bitcast(FP4X4),
+                    lhsT_scale=w4_plane[:, P * m : P * (m + 1)],
+                    rhs=got_words[:, j : j + step].bitcast(FP8X4),
+                    rhs_scale=got_plane[:, j : j + step],
+                    start=(j == lo),
+                    stop=False,
+                )
+            nc.tensor.matmul_mx(
+                out=acc[:],
+                lhsT=u_q[0][:].bitcast(FP8X4),
+                lhsT_scale=u_q[1][:],
+                rhs=c_q[0][:].bitcast(FP8X4),
+                rhs_scale=c_q[1][:],
+                start=False,
+                stop=True,
+            )
+            y = keep.tile([P, hi - lo], F32, name="y%d_%d" % (m, n), align_bytes=64)
+            nc.scalar.activation(out=y[:], in_=acc[:], func=ident, bias=bias[:, m : m + 1])
+            return y
+
+        def scatter(m, n, y):
+            lo, hi = CHUNKS[n]
+            w = wgo_a[:] if n == 0 else wgo_b[:, lo - 256 : hi - 256]
+            nc.vector.tensor_tensor(pages[m][:].indirect(idx2[:, lo // 16 : hi // 16]), y[:], w, mult)
+
+        gather(*GATHERS[0])
+        u0 = quantize("u0", u_raw[:, :, 0:P], P)
+        c0 = quantize("c0", c_raw[0][:], 256)
+        gather(*GATHERS[1])
+        y00 = project(0, 0, u0, c0)
+        u1 = quantize("u1", u_raw[:, :, P:M], P)
+        y10 = project(1, 0, u1, c0)
+        c1 = quantize("c1", c_raw[1][:], 256)
+        scatter(0, 0, y00)
+        scatter(1, 0, y10)
+        y01 = project(0, 1, u0, c1)
+        y11 = project(1, 1, u1, c1)
+        c2 = quantize("c2", c_raw[2][:], 512)
+        scatter(0, 1, y01)
+        scatter(1, 1, y11)
+        y02 = project(0, 2, u0, c2)
+        y12 = project(1, 2, u1, c2)
+        scatter(0, 2, y02)
+        nc.sync.dma_start(out=out[0:P, :], in_=pages[0][:])
+        scatter(1, 2, y12)
+        nc.sync.dma_start(out=out[P:M, :], in_=pages[1][:])

@@ -17,15 +17,7 @@ FP4X4 = mybir.dt.float4_e2m1fn_x4
 P = 128
 PACK = 4
 QUADS = 4
-CHUNKS = [(0, 256), (256, 512), (512, 1024)]
-GATHERS = [(0, 256), (256, 1024)]
-
-
-def interleave(nc, grouped, raw):
-    nc.scalar.copy(
-        out=grouped.rearrange("p (c i) t -> p c t i", i=4),
-        in_=raw.rearrange("p t (c i) -> p c t i", i=4),
-    )
+Q = 256
 
 
 def tile_list_tabscat_d_bias_kernel(tc, tab, w4_words, w4_scales, c, u, b, wgo, offs, offs2, out):
@@ -36,119 +28,132 @@ def tile_list_tabscat_d_bias_kernel(tc, tab, w4_words, w4_scales, c, u, b, wgo, 
         keep = ctx.enter_context(tc.tile_pool(name="keep", bufs=1))
         psum = ctx.enter_context(tc.psum_pool(name="psum", bufs=1))
 
+        def sb(name, shape, dtype, tag=None):
+            return keep.tile(shape, dtype, name=name, tag=tag or name, align_bytes=64)
+
         idx = keep.tile([P, S // 16], U16, name="idx")
         idx2 = keep.tile([P, S // 16], U16, name="idx2")
-        tab_words = keep.tile([P, T], I32, name="tab_words", align_bytes=64)
-        tab_plane = keep.tile([P, T], U8, name="tab_plane", align_bytes=64)
-        w4_codes = keep.tile([P, 2 * M], U8, name="w4_codes", align_bytes=64)
-        w4_plane = keep.tile([P, M], U8, name="w4_plane", align_bytes=64)
-        bias = keep.tile([P, 2], F32, name="bias")
-        u_raw = keep.tile([P, PACK, M], F32, name="u_raw", align_bytes=64)
-        pages = [keep.tile([P, T], F32, name="page%d" % m, align_bytes=64) for m in range(2)]
-
-        nc.vector.memset(tab_plane[:].bitcast(I32), 0)
-        nc.vector.memset(w4_plane[:].bitcast(I32), 0)
-        for page in pages:
-            nc.vector.memset(page[:], 0.0)
+        tab_words = sb("tab_words", [P, T], I32)
+        tab_plane = sb("tab_plane", [P, T], U8)
+        w4_codes = sb("w4_codes", [P, 2 * M], U8)
+        w4_plane = sb("w4_plane", [P, M], U8)
+        bias = sb("bias", [P, 2], F32)
+        u_raw = sb("u_raw", [P, PACK, M], F32)
+        pages = [sb("page%d" % m, [P, T], F32) for m in range(2)]
+        c_raw = [sb("c_raw%d" % n, [P, PACK, Q], F32) for n in range(4)]
+        wgo_a = sb("wgo_a", [P, Q], F32)
+        wgo_b = sb("wgo_b", [P, S - Q], F32)
 
         tab_i32 = tab[0].bitcast(I32)
         tab_rows = tab_i32[P * T :].rearrange("(q r t) -> r q t", q=QUADS, r=4)
         w4_rows = w4_scales[0].bitcast(I32).rearrange("(q r) n -> r q n", q=QUADS)
         c_view = c.rearrange("(p t) j -> p t j", t=PACK)
 
-        with nc.allow_non_contiguous_dma(reason="one bias value for each partition"):
-            nc.gpsimd.dma_start(out=bias[:], in_=b.rearrange("(m p) -> p m", p=P))
-        nc.gpsimd.dma_start(out=w4_codes[:].bitcast(I32), in_=w4_words[0].bitcast(I32))
+        def load_c(n):
+            nc.sync.dma_start(out=c_raw[n][:], in_=c_view[:, :, n * Q : (n + 1) * Q])
 
+        nc.vector.memset(tab_plane[:].bitcast(I32), 0)
+        for page in pages:
+            nc.vector.memset(page[:].bitcast(I32), 0)
+        nc.gpsimd.dma_start(out=w4_codes[:].bitcast(I32), in_=w4_words[0].bitcast(I32))
+        with nc.allow_non_contiguous_dma(reason="one bias value for each partition"):
+            nc.scalar.dma_start(out=bias[:], in_=b.rearrange("(m p) -> p m", p=P))
         nc.sync.dma_start(idx[:], offs)
         nc.sync.dma_start(out=tab_words[:], in_=tab_i32[: P * T].rearrange("(p t) -> p t", p=P))
         for r in range(4):
             nc.sync.dma_start(out=tab_plane[r:P:32, :].bitcast(I32), in_=tab_rows[r])
         nc.sync.dma_start(out=u_raw[:], in_=u.rearrange("(p t) n -> p t n", t=PACK))
-        c_raw = []
-        for n, (lo, hi) in enumerate(CHUNKS):
-            c_raw.append(keep.tile([P, PACK, hi - lo], F32, name="c_raw%d" % n, align_bytes=64))
-        wgo_a = keep.tile([P, 256], F32, name="wgo_a", align_bytes=64)
-        wgo_b = keep.tile([P, S - 256], F32, name="wgo_b", align_bytes=64)
-        nc.sync.dma_start(out=c_raw[0][:], in_=c_view[:, :, 0:256])
-        nc.sync.dma_start(idx2[:], offs2)
-        nc.sync.dma_start(out=wgo_a[:], in_=wgo[:, 0:256])
+        load_c(0)
+        load_c(1)
         for r in range(4):
             nc.sync.dma_start(out=w4_plane[r:P:32, :].bitcast(I32), in_=w4_rows[r])
-        nc.sync.dma_start(out=c_raw[1][:], in_=c_view[:, :, 256:512])
-        nc.sync.dma_start(out=wgo_b[:], in_=wgo[:, 256:S])
-        nc.sync.dma_start(out=c_raw[2][:], in_=c_view[:, :, 512:S])
+        nc.sync.dma_start(idx2[:], offs2)
+        nc.sync.dma_start(out=wgo_a[:], in_=wgo[:, 0:Q])
+        load_c(2)
+        load_c(3)
+        nc.sync.dma_start(out=wgo_b[:], in_=wgo[:, Q:S])
 
-        got_words = keep.tile([P, S], U32, name="got_words", align_bytes=64)
-        got_plane = keep.tile([P, S], U8, name="got_plane", align_bytes=64)
+        def gather_words(name, lo, hi):
+            got = sb(name, [P, hi - lo], U32)
+            nc.vector.tensor_copy(got[:], tab_words[:].bitcast(U32).indirect(idx[:, lo // 16 : hi // 16]))
+            return got
 
-        def gather(lo, hi):
-            part = idx[:, lo // 16 : hi // 16]
-            nc.vector.tensor_copy(got_words[:, lo:hi], tab_words[:].bitcast(U32).indirect(part))
-            nc.vector.tensor_copy(got_plane[:, lo:hi], tab_plane[:].indirect(part))
+        def gather_plane(name, lo, hi, tag=None):
+            got = sb(name, [P, hi - lo], U8, tag)
+            nc.vector.tensor_copy(got[:], tab_plane[:].indirect(idx[:, lo // 16 : hi // 16]))
+            return got
 
-        def quantize(name, raw, width):
-            grouped = keep.tile([P, width, PACK], BF16, name=name + "_bf", align_bytes=64)
-            codes = keep.tile([P, width], U32, name=name + "_codes", align_bytes=64)
-            plane = keep.tile([P, width], U8, name=name + "_plane", align_bytes=64)
-            for lo in range(0, width, 256):
-                hi = min(lo + 256, width)
-                interleave(nc, grouped[:, lo:hi, :], raw[:, :, lo:hi])
+        def quantize(name, raw, width, tag=None):
+            grouped = sb(name + "_bf", [P, width, PACK], BF16, tag)
+            codes = sb(name + "_codes", [P, width], U32)
+            plane = sb(name + "_plane", [P, width], U8)
+            nc.scalar.copy(
+                out=grouped[:].rearrange("p (c i) t -> p c t i", i=4),
+                in_=raw.rearrange("p t (c i) -> p c t i", i=4),
+            )
             nc.vector.quantize_mx(
                 out=codes[:].bitcast(FP8X4), scales=plane[:], in_=grouped[:].rearrange("p w t -> p (w t)")
             )
             return codes, plane
 
-        def project(m, n, u_q, c_q):
-            lo, hi = CHUNKS[n]
-            acc = psum.tile([P, hi - lo], F32, name="acc%d_%d" % (m, n))
-            step = 512 if hi - lo == 512 else 128
-            for j in range(lo, hi, step):
+        def project(name, m, words, plane, u_q, c_qs):
+            width = Q * len(c_qs)
+            acc = psum.tile([P, width], F32, name="acc" + name)
+            step = 512 if width == 512 else 128
+            for j in range(0, width, step):
                 nc.tensor.matmul_mx(
-                    out=acc[:, j - lo : j - lo + step],
+                    out=acc[:, j : j + step],
                     lhsT=w4_codes[:, 2 * P * m : 2 * P * (m + 1)].bitcast(FP4X4),
                     lhsT_scale=w4_plane[:, P * m : P * (m + 1)],
-                    rhs=got_words[:, j : j + step].bitcast(FP8X4),
-                    rhs_scale=got_plane[:, j : j + step],
-                    start=(j == lo),
+                    rhs=words[:, j : j + step].bitcast(FP8X4),
+                    rhs_scale=plane[:, j : j + step],
+                    start=(j == 0),
                     stop=False,
                 )
-            nc.tensor.matmul_mx(
-                out=acc[:],
-                lhsT=u_q[0][:].bitcast(FP8X4),
-                lhsT_scale=u_q[1][:],
-                rhs=c_q[0][:].bitcast(FP8X4),
-                rhs_scale=c_q[1][:],
-                start=False,
-                stop=True,
-            )
-            y = keep.tile([P, hi - lo], F32, name="y%d_%d" % (m, n), align_bytes=64)
+            for n, c_q in enumerate(c_qs):
+                nc.tensor.matmul_mx(
+                    out=acc[:, n * Q : (n + 1) * Q],
+                    lhsT=u_q[0][:].bitcast(FP8X4),
+                    lhsT_scale=u_q[1][:],
+                    rhs=c_q[0][:].bitcast(FP8X4),
+                    rhs_scale=c_q[1][:],
+                    start=False,
+                    stop=(n == len(c_qs) - 1),
+                )
+            return acc
+
+        def evac(name, m, acc, tag=None):
+            y = sb("y" + name, [P, acc.shape[1]], F32, tag)
             nc.scalar.activation(out=y[:], in_=acc[:], func=ident, bias=bias[:, m : m + 1])
             return y
 
-        def scatter(m, n, y):
-            lo, hi = CHUNKS[n]
-            w = wgo_a[:] if n == 0 else wgo_b[:, lo - 256 : hi - 256]
+        def scatter(m, lo, hi, y):
+            w = wgo_a[:] if lo == 0 else wgo_b[:, lo - Q : hi - Q]
             nc.vector.tensor_tensor(pages[m][:].indirect(idx2[:, lo // 16 : hi // 16]), y[:], w, mult)
 
-        gather(*GATHERS[0])
+        words_a = gather_words("words_a", 0, Q)
+        plane_a = gather_plane("plane_a", 0, Q)
+        words_b = gather_words("words_b", Q, S)
+        plane_b = gather_plane("plane_b", Q, 2 * Q)
         u0 = quantize("u0", u_raw[:, :, 0:P], P)
-        c0 = quantize("c0", c_raw[0][:], 256)
-        gather(*GATHERS[1])
-        y00 = project(0, 0, u0, c0)
-        u1 = quantize("u1", u_raw[:, :, P:M], P)
-        y10 = project(1, 0, u1, c0)
-        c1 = quantize("c1", c_raw[1][:], 256)
-        scatter(0, 0, y00)
-        scatter(1, 0, y10)
-        y01 = project(0, 1, u0, c1)
-        y11 = project(1, 1, u1, c1)
-        c2 = quantize("c2", c_raw[2][:], 512)
-        scatter(0, 1, y01)
-        scatter(1, 1, y11)
-        y02 = project(0, 2, u0, c2)
-        y12 = project(1, 2, u1, c2)
-        scatter(0, 2, y02)
+        c0 = quantize("c0", c_raw[0][:], Q)
+        plane_c = gather_plane("plane_c", 2 * Q, S, "c0_bf")
+        y0a = evac("0a", 0, project("0a", 0, words_a, plane_a, u0, [c0]))
+        u1 = quantize("u1", u_raw[:, :, P:M], P, "c_raw0")
+        scatter(0, 0, Q, y0a)
+        acc1a = project("1a", 1, words_a, plane_a, u1, [c0])
+        c1 = quantize("c1", c_raw[1][:], Q, "c0_codes")
+        y1a = evac("1a", 1, acc1a, "c_raw1")
+        scatter(1, 0, Q, y1a)
+        c2 = quantize("c2", c_raw[2][:], Q)
+        y0b = evac("0b", 0, project("0b", 0, words_b[:, 0:Q], plane_b, u0, [c1]), "c_raw2")
+        scatter(0, Q, 2 * Q, y0b)
+        c3 = quantize("c3", c_raw[3][:], Q)
+        y1b = evac("1b", 1, project("1b", 1, words_b[:, 0:Q], plane_b, u1, [c1]), "c_raw3")
+        scatter(1, Q, 2 * Q, y1b)
+        y0c = evac("0c", 0, project("0c", 0, words_b[:, Q:], plane_c, u0, [c2, c3]))
+        y1c = evac("1c", 1, project("1c", 1, words_b[:, Q:], plane_c, u1, [c2, c3]))
+        scatter(0, 2 * Q, S, y0c)
         nc.sync.dma_start(out=out[0:P, :], in_=pages[0][:])
-        scatter(1, 2, y12)
+        scatter(1, 2 * Q, S, y1c)
         nc.sync.dma_start(out=out[P:M, :], in_=pages[1][:])

@@ -55,23 +55,23 @@ def tile_list_tabscat_d_bias_kernel(tc, tab, w4_words, w4_scales, c, u, b, wgo, 
         nc.vector.memset(tab_plane[:].bitcast(I32), 0)
         for page in pages:
             nc.vector.memset(page[:].bitcast(I32), 0)
-        nc.gpsimd.dma_start(out=w4_codes[:].bitcast(I32), in_=w4_words[0].bitcast(I32))
         with nc.allow_non_contiguous_dma(reason="one bias value for each partition"):
             nc.scalar.dma_start(out=bias[:], in_=b.rearrange("(m p) -> p m", p=P))
         nc.sync.dma_start(idx[:], offs)
-        nc.sync.dma_start(out=tab_words[:], in_=tab_i32[: P * T].rearrange("(p t) -> p t", p=P))
+        load_c(0)
         for r in range(4):
             nc.sync.dma_start(out=tab_plane[r:P:32, :].bitcast(I32), in_=tab_rows[r])
         nc.sync.dma_start(out=u_raw[:], in_=u.rearrange("(p t) n -> p t n", t=PACK))
-        load_c(0)
-        load_c(1)
+        nc.sync.dma_start(out=tab_words[:], in_=tab_i32[: P * T].rearrange("(p t) -> p t", p=P))
+        nc.sync.dma_start(out=w4_codes[:].bitcast(I32), in_=w4_words[0].bitcast(I32))
         for r in range(4):
             nc.sync.dma_start(out=w4_plane[r:P:32, :].bitcast(I32), in_=w4_rows[r])
         nc.sync.dma_start(idx2[:], offs2)
+        load_c(1)
         nc.sync.dma_start(out=wgo_a[:], in_=wgo[:, 0:Q])
         load_c(2)
-        load_c(3)
         nc.sync.dma_start(out=wgo_b[:], in_=wgo[:, Q:S])
+        load_c(3)
 
         def gather_words(name, lo, hi):
             got = sb(name, [P, hi - lo], U32)
@@ -96,29 +96,34 @@ def tile_list_tabscat_d_bias_kernel(tc, tab, w4_words, w4_scales, c, u, b, wgo, 
             )
             return codes, plane
 
-        def project(name, m, words, plane, u_q, c_qs):
+        def project(name, m, words, plane, u_q, c_qs, dense_first=False):
             width = Q * len(c_qs)
             acc = psum.tile([P, width], F32, name="acc" + name)
             step = 512 if width == 512 else 128
-            for j in range(0, width, step):
-                nc.tensor.matmul_mx(
-                    out=acc[:, j : j + step],
-                    lhsT=w4_codes[:, 2 * P * m : 2 * P * (m + 1)].bitcast(FP4X4),
-                    lhsT_scale=w4_plane[:, P * m : P * (m + 1)],
-                    rhs=words[:, j : j + step].bitcast(FP8X4),
-                    rhs_scale=plane[:, j : j + step],
-                    start=(j == 0),
-                    stop=False,
+            table = [
+                (
+                    acc[:, j : j + step],
+                    w4_codes[:, 2 * P * m : 2 * P * (m + 1)].bitcast(FP4X4),
+                    w4_plane[:, P * m : P * (m + 1)],
+                    words[:, j : j + step].bitcast(FP8X4),
+                    plane[:, j : j + step],
                 )
-            for n, c_q in enumerate(c_qs):
+                for j in range(0, width, step)
+            ]
+            dense = [
+                (acc[:, n * Q : (n + 1) * Q], u_q[0][:].bitcast(FP8X4), u_q[1][:], c_q[0][:].bitcast(FP8X4), c_q[1][:])
+                for n, c_q in enumerate(c_qs)
+            ]
+            passes = dense + table if dense_first else table + dense
+            for n, (dst, lhs, lhs_scale, rhs, rhs_scale) in enumerate(passes):
                 nc.tensor.matmul_mx(
-                    out=acc[:, n * Q : (n + 1) * Q],
-                    lhsT=u_q[0][:].bitcast(FP8X4),
-                    lhsT_scale=u_q[1][:],
-                    rhs=c_q[0][:].bitcast(FP8X4),
-                    rhs_scale=c_q[1][:],
-                    start=False,
-                    stop=(n == len(c_qs) - 1),
+                    out=dst,
+                    lhsT=lhs,
+                    lhsT_scale=lhs_scale,
+                    rhs=rhs,
+                    rhs_scale=rhs_scale,
+                    start=(n == 0),
+                    stop=(n == len(passes) - 1),
                 )
             return acc
 
@@ -131,28 +136,26 @@ def tile_list_tabscat_d_bias_kernel(tc, tab, w4_words, w4_scales, c, u, b, wgo, 
             w = wgo_a[:] if lo == 0 else wgo_b[:, lo - Q : hi - Q]
             nc.vector.tensor_tensor(pages[m][:].indirect(idx2[:, lo // 16 : hi // 16]), y[:], w, mult)
 
-        words_a = gather_words("words_a", 0, Q)
-        plane_a = gather_plane("plane_a", 0, Q)
-        words_b = gather_words("words_b", Q, S)
-        plane_b = gather_plane("plane_b", Q, 2 * Q)
-        u0 = quantize("u0", u_raw[:, :, 0:P], P)
+        plane = gather_plane("plane", 0, S)
         c0 = quantize("c0", c_raw[0][:], Q)
-        plane_c = gather_plane("plane_c", 2 * Q, S, "c0_bf")
-        y0a = evac("0a", 0, project("0a", 0, words_a, plane_a, u0, [c0]))
-        u1 = quantize("u1", u_raw[:, :, P:M], P, "c_raw0")
+        u0 = quantize("u0", u_raw[:, :, 0:P], P)
+        u1 = quantize("u1", u_raw[:, :, P:M], P)
+        words_a = gather_words("words_a", 0, Q)
+        words_b = gather_words("words_b", Q, S)
+        y0a = evac("0a", 0, project("0a", 0, words_a, plane[:, 0:Q], u0, [c0], True))
         scatter(0, 0, Q, y0a)
-        acc1a = project("1a", 1, words_a, plane_a, u1, [c0])
+        acc1a = project("1a", 1, words_a, plane[:, 0:Q], u1, [c0], True)
         c1 = quantize("c1", c_raw[1][:], Q, "c0_codes")
         y1a = evac("1a", 1, acc1a, "c_raw1")
         scatter(1, 0, Q, y1a)
         c2 = quantize("c2", c_raw[2][:], Q)
-        y0b = evac("0b", 0, project("0b", 0, words_b[:, 0:Q], plane_b, u0, [c1]), "c_raw2")
+        y0b = evac("0b", 0, project("0b", 0, words_b[:, 0:Q], plane[:, Q : 2 * Q], u0, [c1]), "c_raw2")
         scatter(0, Q, 2 * Q, y0b)
         c3 = quantize("c3", c_raw[3][:], Q)
-        y1b = evac("1b", 1, project("1b", 1, words_b[:, 0:Q], plane_b, u1, [c1]), "c_raw3")
+        y1b = evac("1b", 1, project("1b", 1, words_b[:, 0:Q], plane[:, Q : 2 * Q], u1, [c1]), "c_raw3")
         scatter(1, Q, 2 * Q, y1b)
-        y0c = evac("0c", 0, project("0c", 0, words_b[:, Q:], plane_c, u0, [c2, c3]))
-        y1c = evac("1c", 1, project("1c", 1, words_b[:, Q:], plane_c, u1, [c2, c3]))
+        y0c = evac("0c", 0, project("0c", 0, words_b[:, Q:], plane[:, 2 * Q :], u0, [c2, c3]))
+        y1c = evac("1c", 1, project("1c", 1, words_b[:, Q:], plane[:, 2 * Q :], u1, [c2, c3]))
         scatter(0, 2 * Q, S, y0c)
         nc.sync.dma_start(out=out[0:P, :], in_=pages[0][:])
         scatter(1, 2 * Q, S, y1c)

from contextlib import ExitStack

import concourse.mybir as mybir

K, M, T, S = 512, 256, 2048, 1024
FLOPS = 2 * 2 * K * M * S

F32 = mybir.dt.float32
BF16 = mybir.dt.bfloat16
I32 = mybir.dt.int32
U32 = mybir.dt.uint32
U16 = mybir.dt.uint16
U8 = mybir.dt.uint8
FP8X4 = mybir.dt.float8_e4m3fn_x4
FP4X4 = mybir.dt.float4_e2m1fn_x4

P = 128
PACK = 4
QUADS = 4
Q = 256


def tile_list_tabscat_d_bias_kernel(tc, tab, w4_words, w4_scales, c, u, b, wgo, offs, offs2, out):
    nc = tc.nc
    mult = mybir.AluOpType.mult
    ident = mybir.ActivationFunctionType.Identity
    with ExitStack() as ctx:
        keep = ctx.enter_context(tc.tile_pool(name="keep", bufs=1))
        psum = ctx.enter_context(tc.psum_pool(name="psum", bufs=1))

        def sb(name, shape, dtype, tag=None):
            return keep.tile(shape, dtype, name=name, tag=tag or name, align_bytes=64)

        idx = keep.tile([P, S // 16], U16, name="idx")
        idx2 = keep.tile([P, S // 16], U16, name="idx2")
        tab_words = sb("tab_words", [P, T], I32)
        tab_plane = sb("tab_plane", [P, T], U8)
        w4_codes = sb("w4_codes", [P, 2 * M], U8)
        w4_plane = sb("w4_plane", [P, M], U8)
        bias = sb("bias", [P, 2], F32)
        u_raw = sb("u_raw", [P, PACK, M], F32)
        pages = [sb("page%d" % m, [P, T], F32) for m in range(2)]
        c_raw = [sb("c_raw%d" % n, [P, PACK, Q], F32) for n in range(4)]
        wgo_a = sb("wgo_a", [P, Q], F32)
        wgo_b = sb("wgo_b", [P, S - Q], F32)

        tab_i32 = tab[0].bitcast(I32)
        tab_rows = tab_i32[P * T :].rearrange("(q r t) -> r q t", q=QUADS, r=4)
        w4_rows = w4_scales[0].bitcast(I32).rearrange("(q r) n -> r q n", q=QUADS)
        c_view = c.rearrange("(p t) j -> p t j", t=PACK)

        def load_c(n):
            nc.sync.dma_start(out=c_raw[n][:], in_=c_view[:, :, n * Q : (n + 1) * Q])

        nc.vector.memset(tab_plane[:].bitcast(I32), 0)
        for page in pages:
            nc.vector.memset(page[:].bitcast(I32), 0)
        with nc.allow_non_contiguous_dma(reason="one bias value for each partition"):
            nc.scalar.dma_start(out=bias[:], in_=b.rearrange("(m p) -> p m", p=P))
        nc.sync.dma_start(idx[:], offs)
        load_c(0)
        for r in range(4):
            nc.sync.dma_start(out=tab_plane[r:P:32, :].bitcast(I32), in_=tab_rows[r])
        nc.sync.dma_start(out=u_raw[:], in_=u.rearrange("(p t) n -> p t n", t=PACK))
        nc.sync.dma_start(out=tab_words[:], in_=tab_i32[: P * T].rearrange("(p t) -> p t", p=P))
        nc.sync.dma_start(out=w4_codes[:].bitcast(I32), in_=w4_words[0].bitcast(I32))
        for r in range(4):
            nc.sync.dma_start(out=w4_plane[r:P:32, :].bitcast(I32), in_=w4_rows[r])
        nc.sync.dma_start(idx2[:], offs2)
        load_c(1)
        nc.sync.dma_start(out=wgo_a[:], in_=wgo[:, 0:Q])
        load_c(2)
        nc.sync.dma_start(out=wgo_b[:], in_=wgo[:, Q:S])
        load_c(3)

        def gather_words(name, lo, hi):
            got = sb(name, [P, hi - lo], U32)
            nc.vector.tensor_copy(got[:], tab_words[:].bitcast(U32).indirect(idx[:, lo // 16 : hi // 16]))
            return got

        def gather_plane(name, lo, hi, tag=None):
            got = sb(name, [P, hi - lo], U8, tag)
            nc.vector.tensor_copy(got[:], tab_plane[:].indirect(idx[:, lo // 16 : hi // 16]))
            return got

        def quantize(name, raw, width, tag=None):
            grouped = sb(name + "_bf", [P, width, PACK], BF16, tag)
            codes = sb(name + "_codes", [P, width], U32)
            plane = sb(name + "_plane", [P, width], U8)
            nc.scalar.copy(
                out=grouped[:].rearrange("p (c i) t -> p c t i", i=4),
                in_=raw.rearrange("p t (c i) -> p c t i", i=4),
            )
            nc.vector.quantize_mx(
                out=codes[:].bitcast(FP8X4), scales=plane[:], in_=grouped[:].rearrange("p w t -> p (w t)")
            )
            return codes, plane

        def project(name, m, words, plane, u_q, c_qs, dense_first=False):
            width = Q * len(c_qs)
            acc = psum.tile([P, width], F32, name="acc" + name)
            step = 512 if width == 512 else 128
            table = [
                (
                    acc[:, j : j + step],
                    w4_codes[:, 2 * P * m : 2 * P * (m + 1)].bitcast(FP4X4),
                    w4_plane[:, P * m : P * (m + 1)],
                    words[:, j : j + step].bitcast(FP8X4),
                    plane[:, j : j + step],
                )
                for j in range(0, width, step)
            ]
            dense = [
                (acc[:, n * Q : (n + 1) * Q], u_q[0][:].bitcast(FP8X4), u_q[1][:], c_q[0][:].bitcast(FP8X4), c_q[1][:])
                for n, c_q in enumerate(c_qs)
            ]
            passes = dense + table if dense_first else table + dense
            for n, (dst, lhs, lhs_scale, rhs, rhs_scale) in enumerate(passes):
                nc.tensor.matmul_mx(
                    out=dst,
                    lhsT=lhs,
                    lhsT_scale=lhs_scale,
                    rhs=rhs,
                    rhs_scale=rhs_scale,
                    start=(n == 0),
                    stop=(n == len(passes) - 1),
                )
            return acc

        def evac(name, m, acc, tag=None):
            y = sb("y" + name, [P, acc.shape[1]], F32, tag)
            nc.scalar.activation(out=y[:], in_=acc[:], func=ident, bias=bias[:, m : m + 1])
            return y

        def scatter(m, lo, hi, y):
            w = wgo_a[:] if lo == 0 else wgo_b[:, lo - Q : hi - Q]
            nc.vector.tensor_tensor(pages[m][:].indirect(idx2[:, lo // 16 : hi // 16]), y[:], w, mult)

        plane = gather_plane("plane", 0, S)
        c0 = quantize("c0", c_raw[0][:], Q)
        u0 = quantize("u0", u_raw[:, :, 0:P], P)
        u1 = quantize("u1", u_raw[:, :, P:M], P)
        words_a = gather_words("words_a", 0, Q)
        words_b = gather_words("words_b", Q, S)
        y0a = evac("0a", 0, project("0a", 0, words_a, plane[:, 0:Q], u0, [c0], True))
        scatter(0, 0, Q, y0a)
        acc1a = project("1a", 1, words_a, plane[:, 0:Q], u1, [c0], True)
        c1 = quantize("c1", c_raw[1][:], Q, "c0_codes")
        y1a = evac("1a", 1, acc1a, "c_raw1")
        scatter(1, 0, Q, y1a)
        c2 = quantize("c2", c_raw[2][:], Q)
        y0b = evac("0b", 0, project("0b", 0, words_b[:, 0:Q], plane[:, Q : 2 * Q], u0, [c1]), "c_raw2")
        scatter(0, Q, 2 * Q, y0b)
        c3 = quantize("c3", c_raw[3][:], Q)
        y1b = evac("1b", 1, project("1b", 1, words_b[:, 0:Q], plane[:, Q : 2 * Q], u1, [c1]), "c_raw3")
        scatter(1, Q, 2 * Q, y1b)
        y0c = evac("0c", 0, project("0c", 0, words_b[:, Q:], plane[:, 2 * Q :], u0, [c2, c3]))
        y1c = evac("1c", 1, project("1c", 1, words_b[:, Q:], plane[:, 2 * Q :], u1, [c2, c3]))
        scatter(0, 2 * Q, S, y0c)
        nc.sync.dma_start(out=out[0:P, :], in_=pages[0][:])
        scatter(1, 2 * Q, S, y1c)
        nc.sync.dma_start(out=out[P:M, :], in_=pages[1][:])
